import numpy as np
import ml_dtypes


def mxq(x, axis, fmt="e4m3"):
    dtype, down = {"e4m3": (ml_dtypes.float8_e4m3fn, 7), "e5m2": (ml_dtypes.float8_e5m2, 14)}[fmt]
    v = np.moveaxis(np.asarray(x, np.float32).astype(ml_dtypes.bfloat16).astype(np.float64), axis, -1)
    blocks = v.reshape(v.shape[:-1] + (-1, 32))
    amax = np.abs(blocks).max(-1, keepdims=True)
    byte = np.maximum(np.where(amax > 0, np.frexp(amax)[1] - 1 + 127, 0) - down, 1)
    scale = np.exp2(byte - 127.0)
    codes = (blocks / scale).astype(np.float32).astype(dtype).astype(np.float64)
    return np.moveaxis((codes * scale).reshape(v.shape), -1, axis)


WIDE = False


def mx_kscale(k):
    if not WIDE:
        return np.ones(k)
    levels = np.array([10, -10, 5, -5, 0])
    if k % 512:
        return np.exp2(np.random.permutation(np.resize(levels, k // 32))).repeat(32)
    a = np.empty((k // 512, 16))
    for p in range(k // 512):
        a[p, :8] = np.random.permutation(np.resize(levels, 8))
        for g in range(8):
            far = levels[np.abs(levels - a[p, g]) >= 10]
            a[p, g + 8] = far[np.random.randint(len(far))]
    return np.exp2(a.ravel()).repeat(32)


def f64(x):
    return np.asarray(x).astype(np.float64)


def striped(idx):
    return np.tile(idx.reshape(-1, 16).T, (8, 1)).astype(np.uint16)


def unstriped(offs):
    return offs[:16].T.reshape(-1).astype(np.int64)


def striped8(idx):
    return np.concatenate([x.reshape(-1, 16).T for x in idx]).astype(np.uint16)


def runs(offs, k):
    lists = np.stack([offs[16 * r : 16 * r + 16].T.reshape(-1) for r in range(8)]).astype(np.int64)
    return lists[np.arange(k) % 512 // 64]


def pack_weight(w):
    k, n = w.shape
    w = f64(np.asarray(w, np.float32).astype(ml_dtypes.bfloat16)).reshape(k // 32, 32, n)
    amax = np.abs(w).max(1)
    byte = np.clip(np.where(amax > 0, np.frexp(amax)[1] - 1 + 127 - 7, 1), 1, 254)
    scaled = (w * np.exp2(127.0 - byte)[:, None, :]).reshape(k, n).astype(np.float32)
    words = np.ascontiguousarray(scaled.reshape(k // 512, 128, 4, n).transpose(0, 1, 3, 2)).astype(ml_dtypes.float8_e4m3fn).view(np.uint8)
    return words, np.ascontiguousarray(byte.astype(np.uint8).reshape(k // 512, 16, n))


def unpack_weight(words, scales):
    g, p, n, _ = words.shape
    vals = np.ascontiguousarray(words).view(ml_dtypes.float8_e4m3fn).astype(np.float64) * np.repeat(np.exp2(scales.astype(np.float64) - 127.0), 8, axis=1)[..., None]
    return vals.transpose(0, 1, 3, 2).reshape(g * 512, n)


K, T, S, H, G, U = 512, 2048, 256, 512, 2048, 512


def setup_inputs():
    n = np.random.standard_normal
    s = mx_kscale(K)[:, None]
    packed_xT = pack_weight(n((K, T)) * s)
    packed_dT = pack_weight(n((K, G)) / s)
    perm = np.random.permutation(U)
    return {
        "x_words": packed_xT[0],
        "x_scales": packed_xT[1],
        "w1": (n((K, H)) / np.sqrt(K) / s).astype(np.float32),
        "gs": (np.random.uniform(0.5, 1.5, (K, 1)) * s).astype(np.float32),
        "d_words": packed_dT[0],
        "d_scales": packed_dT[1],
        "offs": striped8(np.random.randint(0, T, (8, S))),
        "n1": striped(np.random.permutation(S)),
        "ka": striped8(np.random.randint(0, G, (8, H))),
        "kb": striped8(np.random.randint(0, G, (8, H))),
        "n2": striped(perm[:S]),
        "n3": striped(perm[S:]),
        "n4": striped(np.random.permutation(S)),
    }


def reference(x_words, x_scales, w1, gs, d_words, d_scales, offs, n1, ka, kb, n2, n3, n4):
    d_ka = unpack_weight(d_words, d_scales)[np.arange(K)[:, None], runs(ka, K)]
    xq = unpack_weight(x_words, x_scales)[np.arange(K)[:, None], runs(offs, K)]
    y = mxq(f64(w1), 0, "e4m3").T @ xq
    ds = np.zeros((H, S))
    ds[:, unstriped(n1)] = y
    z = f64(gs) * (y - ds)
    zq = mxq(z, 0, "e4m3")
    d_kb = unpack_weight(d_words, d_scales)[np.arange(K)[:, None], runs(kb, K)]
    h = 0.0625 * (d_ka.T @ zq + d_kb.T @ zq)
    dn = np.minimum(h, h[:, unstriped(n4)])
    up = np.maximum(h, h[:, unstriped(n4)])
    ph = np.zeros((H, U))
    ph[:, unstriped(n2)] = up
    out = ph.copy()
    out[:, unstriped(n3)] = dn
    return out

@@ -1,0 +1,173 @@
+from contextlib import ExitStack
+
+import concourse.mybir as mybir
+
+K, T, S, H, G, U = 512, 2048, 256, 512, 2048, 512
+FLOPS = 2 * K * H * S * 3
+
+F32 = mybir.dt.float32
+BF16 = mybir.dt.bfloat16
+I32 = mybir.dt.int32
+U32 = mybir.dt.uint32
+U16 = mybir.dt.uint16
+U8 = mybir.dt.uint8
+FP8X4 = mybir.dt.float8_e4m3fn_x4
+ALU = mybir.AluOpType
+COPY = mybir.ActivationFunctionType.Copy
+
+P = 128
+PACK = 4
+M = 128
+TILES = H // M
+SPARE = 16
+
+
+def tile_picked_hdaqsendmxpagmx_none_p_kernel(tc, x_words, x_scales, w1, gs, d_words, d_scales, offs, n1, ka, kb, n2, n3, n4, out):
+    nc = tc.nc
+    with ExitStack() as ctx:
+        lists = ctx.enter_context(tc.tile_pool(name="lists", bufs=1))
+        keep = ctx.enter_context(tc.tile_pool(name="keep", bufs=1))
+        psum = ctx.enter_context(tc.psum_pool(name="psum", bufs=1))
+
+        def load_list(name, src):
+            t = lists.tile(list(src.shape), U16, name=name)
+            nc.sync.dma_start(t[:], src)
+            return t
+
+        def zeroed_bytes(name, width):
+            t = keep.tile([P, width], U8, name=name, align_bytes=64)
+            nc.vector.memset(t[:].bitcast(I32), 0)
+            return t
+
+        def load_scale_rows(name, src, tag):
+            width = src.shape[2]
+            t = keep.tile([P, width], U8, name=name, tag=tag, align_bytes=64)
+            rows = src[0].bitcast(I32).rearrange("(r b) c -> b r c", b=2)
+            for b in range(2):
+                nc.scalar.dma_start(out=t[:].bitcast(I32)[b:P:2, :], in_=rows[b].unsqueeze(1).to_broadcast([8, 8, width // 4]))
+            return t
+
+        def load_words(queue, name, src, tag):
+            t = keep.tile([P, src.shape[2]], I32, name=name, tag=tag, align_bytes=64)
+            queue.dma_start(out=t[:], in_=src[0].rearrange("p n t -> p (n t)").bitcast(I32))
+            return t
+
+        def place_scale_rows(plane, picked):
+            nc.sync.dma_start(out=plane[:].bitcast(I32)[0:112, :], in_=picked[:].bitcast(I32)[14:126, :])
+
+        offs_t = load_list("offs_t", offs)
+        ka_t = load_list("ka_t", ka)
+        kb_t = load_list("kb_t", kb)
+        n1_t = load_list("n1_t", n1)
+        n4_t = load_list("n4_t", n4)
+        n2_t = load_list("n2_t", n2)
+        n3_t = load_list("n3_t", n3)
+        x_scale_tab = load_scale_rows("x_scale_tab", x_scales, "slot_s")
+        w_raw = keep.tile([P, PACK, H], F32, name="w_raw", tag="slot_w", align_bytes=64)
+        nc.scalar.dma_start(out=w_raw[:], in_=w1.rearrange("(p j) c -> p j c", j=PACK))
+        x_tab = load_words(nc.scalar, "x_tab", x_words, "slot_x")
+        d_scale_tab = load_scale_rows("d_scale_tab", d_scales, "d_scale_tab")
+        gs_t = keep.tile([P, PACK], F32, name="gs_t")
+        nc.gpsimd.dma_start(out=gs_t[:], in_=gs.rearrange("(p t) o -> p (t o)", t=PACK))
+
+        x_plane = zeroed_bytes("x_plane", S)
+        d_plane = zeroed_bytes("d_plane", 2 * H)
+        pages = []
+        for a in range(TILES):
+            page = keep.tile([P, U], F32, name="page%d" % a)
+            nc.vector.memset(page[:], 0.0)
+            pages.append(page)
+
+        x_bytes = keep.tile([P, S], U8, name="x_bytes", align_bytes=64)
+        nc.vector.tensor_copy(x_bytes[:], x_scale_tab[:].indirect(offs_t[:]))
+        place_scale_rows(x_plane, x_bytes)
+
+        w_dealt = w_raw[:].rearrange("p j (m t) -> p m t j", t=PACK)
+        w_codes, w_scales = [], []
+        w_bfs = []
+        for half in range(2):
+            w_bf = keep.tile([P, 2, M, PACK], BF16, name="w_bf%d" % half, tag=("slot_s", "w_bf1")[half], align_bytes=64)
+            dst = w_bf[:].rearrange("p t m j -> p m t j")
+            src = w_dealt[:, :, 2 * half : 2 * half + 2, :]
+            nc.vector.tensor_copy(out=dst, in_=src)
+            w_bfs.append(w_bf)
+
+        d_tab = load_words(nc.sync, "d_tab", d_words, "slot_w")
+
+        def quantise(name, values, width):
+            codes = keep.tile([P, width], U32, name=name + "_codes", align_bytes=64)
+            scales = keep.tile([P, width], U8, name=name + "_scales", align_bytes=64)
+            return codes, scales
+
+        def quantise_w(half):
+            codes, scales = quantise("w%d" % half, None, 2 * M)
+            nc.vector.quantize_mx(out=codes[:].bitcast(FP8X4), scales=scales[:], in_=w_bfs[half][:].rearrange("p t m j -> p (t m j)"))
+            w_codes.append(codes)
+            w_scales.append(scales)
+
+        quantise_w(0)
+        x_codes = keep.tile([P, S], U32, name="x_codes", tag="slot_c", align_bytes=64)
+        nc.vector.tensor_copy(x_codes[:], x_tab[:].bitcast(U32).indirect(offs_t[:]))
+        quantise_w(1)
+
+        ys, sent = [], []
+        for t in range(PACK):
+            acc = psum.tile([P, S], F32, name="y_acc%d" % t)
+            cols = slice((t % 2) * M, (t % 2 + 1) * M)
+            nc.tensor.matmul_mx(out=acc[:], lhsT=w_codes[t // 2][:, cols].bitcast(FP8X4), lhsT_scale=w_scales[t // 2][:, cols],
+                                rhs=x_codes[:].bitcast(FP8X4), rhs_scale=x_plane[:], start=True, stop=True)
+            y = keep.tile([P, S], F32, name="y%d" % t)
+            if t == 0:
+                nc.scalar.activation(y[:], acc[:], COPY, scale=gs_t[:, t : t + 1])
+            else:
+                nc.vector.tensor_scalar(y[:], acc[:], gs_t[:, t : t + 1], None, ALU.mult)
+            ds = keep.tile([P, 2 * S], F32, name="ds%d" % t)
+            nc.scalar.activation(ds[:].indirect(n1_t[:]), y[:], COPY)
+            ys.append(y)
+            sent.append(ds)
+
+        d_bytes = keep.tile([P, 2 * H], U8, name="d_bytes", tag="slot_c", align_bytes=64)
+        nc.vector.tensor_copy(d_bytes[:, 0:H], d_scale_tab[:].indirect(ka_t[:]))
+        nc.vector.tensor_copy(d_bytes[:, H : 2 * H], d_scale_tab[:].indirect(kb_t[:]))
+        place_scale_rows(d_plane, d_bytes)
+        d_codes = keep.tile([P, 2 * H], U32, name="d_codes", tag="d_scale_tab", align_bytes=64)
+        for side, picks in enumerate((ka_t, kb_t)):
+            nc.vector.tensor_copy(d_codes[:, side * H : (side + 1) * H], d_tab[:].bitcast(U32).indirect(picks[:]))
+
+        z_flat = keep.tile([P, PACK, S], BF16, name="z_flat", tag="slot_w", align_bytes=64)
+        z_bf = keep.tile([P, S, PACK], BF16, name="z_bf", align_bytes=64)
+        for t in range(PACK):
+            nc.vector.tensor_tensor(z_flat[:, t, :], ys[t][:], sent[t][:, 0:S], ALU.subtract)
+        nc.vector.tensor_copy(out=z_bf[:].rearrange("p (c i) t -> p c t i", i=4), in_=z_flat[:].rearrange("p t (c i) -> p c t i", i=4))
+        z_codes, z_scales = quantise("z", None, S)
+        nc.vector.quantize_mx(out=z_codes[:].bitcast(FP8X4), scales=z_scales[:], in_=z_bf[:].rearrange("p j t -> p (j t)"))
+
+        for pair in range(TILES // 2):
+            tiles = (2 * pair, 2 * pair + 1)
+            hs, fetched, ups, dns = {}, {}, {}, {}
+            for a in tiles:
+                acc = psum.tile([P, S], F32, name="h_acc%d" % a)
+                for side in range(2):
+                    nc.tensor.matmul_mx(out=acc[:], lhsT=d_codes[:, side * H + a * M : side * H + (a + 1) * M].bitcast(FP8X4),
+                                        lhsT_scale=d_plane[:, side * H + a * M : side * H + (a + 1) * M],
+                                        rhs=z_codes[:].bitcast(FP8X4), rhs_scale=z_scales[:], start=(side == 0), stop=(side == 1))
+                h = keep.tile([P, S + SPARE], F32, name="h%d" % a)
+                if a == 0:
+                    nc.scalar.activation(h[:, 0:S], acc[:], COPY, scale=0.0625)
+                else:
+                    nc.vector.tensor_scalar(h[:, 0:S], acc[:], 0.0625, None, ALU.mult)
+                hs[a] = h
+            for a in tiles:
+                fetched[a] = keep.tile([P, S], F32, name="fetched%d" % a)
+                nc.scalar.activation(fetched[a][:], hs[a][:].indirect(n4_t[:]), COPY)
+            for a in tiles:
+                ups[a] = keep.tile([P, S], F32, name="up%d" % a)
+                nc.vector.tensor_tensor(ups[a][:], hs[a][:, 0:S], fetched[a][:], ALU.max)
+            for a in tiles:
+                dns[a] = keep.tile([P, S], F32, name="dn%d" % a)
+                nc.vector.tensor_tensor(dns[a][:], hs[a][:, 0:S], fetched[a][:], ALU.min)
+            for a in tiles:
+                nc.scalar.activation(pages[a][:].indirect(n2_t[:]), ups[a][:], COPY)
+            for a in tiles:
+                nc.scalar.activation(pages[a][:].indirect(n3_t[:]), dns[a][:], COPY)
+                nc.sync.dma_start(out=out[a * M : (a + 1) * M, :], in_=pages[a][:])

@@ -34,17 +34,12 @@ def tile_picked_hdaqsendmxpagmx_none_p_kernel(tc, x_words, x_scales, w1, gs, d_w
             nc.sync.dma_start(t[:], src)
             return t
 
-        def zeroed_bytes(name, width):
-            t = keep.tile([P, width], U8, name=name, align_bytes=64)
-            nc.vector.memset(t[:].bitcast(I32), 0)
-            return t
-
         def load_scale_rows(name, src, tag):
-            width = src.shape[2]
-            t = keep.tile([P, width], U8, name=name, tag=tag, align_bytes=64)
+            t = keep.tile([P, src.shape[2]], U8, name=name, tag=tag, align_bytes=64)
+            nc.vector.memset(t[:].bitcast(I32), 0)
             rows = src[0].bitcast(I32).rearrange("(r b) c -> b r c", b=2)
             for b in range(2):
-                nc.scalar.dma_start(out=t[:].bitcast(I32)[b:P:2, :], in_=rows[b].unsqueeze(1).to_broadcast([8, 8, width // 4]))
+                nc.gpsimd.dma_start(out=t[:].bitcast(I32)[b:P:16, :], in_=rows[b])
             return t
 
         def load_words(queue, name, src, tag):
@@ -52,8 +47,12 @@ def tile_picked_hdaqsendmxpagmx_none_p_kernel(tc, x_words, x_scales, w1, gs, d_w
             queue.dma_start(out=t[:], in_=src[0].rearrange("p n t -> p (n t)").bitcast(I32))
             return t
 
-        def place_scale_rows(plane, picked):
-            nc.sync.dma_start(out=plane[:].bitcast(I32)[0:112, :], in_=picked[:].bitcast(I32)[14:126, :])
+        def place_scale_rows(name, picked):
+            plane = keep.tile(list(picked.shape), U8, name=name, align_bytes=64)
+            nc.vector.tensor_copy(plane[:].bitcast(I32), picked[:].bitcast(I32))
+            for b in range(2):
+                nc.sync.dma_start(out=plane[:].bitcast(I32)[2 + b : P : 32, :], in_=picked[:].bitcast(I32)[16 + b : P : 32, :])
+            return plane
 
         offs_t = load_list("offs_t", offs)
         ka_t = load_list("ka_t", ka)
@@ -65,42 +64,35 @@ def tile_picked_hdaqsendmxpagmx_none_p_kernel(tc, x_words, x_scales, w1, gs, d_w
         x_scale_tab = load_scale_rows("x_scale_tab", x_scales, "slot_s")
         w_raw = keep.tile([P, PACK, H], F32, name="w_raw", tag="slot_w", align_bytes=64)
         nc.scalar.dma_start(out=w_raw[:], in_=w1.rearrange("(p j) c -> p j c", j=PACK))
+        gs_t = keep.tile([P, PACK], F32, name="gs_t")
+        nc.scalar.dma_start(out=gs_t[:], in_=gs.rearrange("(p t) o -> p (t o)", t=PACK))
         x_tab = load_words(nc.scalar, "x_tab", x_words, "slot_x")
         d_scale_tab = load_scale_rows("d_scale_tab", d_scales, "d_scale_tab")
-        gs_t = keep.tile([P, PACK], F32, name="gs_t")
-        nc.gpsimd.dma_start(out=gs_t[:], in_=gs.rearrange("(p t) o -> p (t o)", t=PACK))
-
-        x_plane = zeroed_bytes("x_plane", S)
-        d_plane = zeroed_bytes("d_plane", 2 * H)
-        pages = []
-        for a in range(TILES):
-            page = keep.tile([P, U], F32, name="page%d" % a)
-            nc.vector.memset(page[:], 0.0)
-            pages.append(page)
+        pages = [keep.tile([P, U], F32, name="page%d" % a) for a in range(TILES)]
 
         x_bytes = keep.tile([P, S], U8, name="x_bytes", align_bytes=64)
         nc.vector.tensor_copy(x_bytes[:], x_scale_tab[:].indirect(offs_t[:]))
-        place_scale_rows(x_plane, x_bytes)
+        x_plane = place_scale_rows("x_plane", x_bytes)
 
         w_dealt = w_raw[:].rearrange("p j (m t) -> p m t j", t=PACK)
         w_codes, w_scales = [], []
         w_bfs = []
         for half in range(2):
-            w_bf = keep.tile([P, 2, M, PACK], BF16, name="w_bf%d" % half, tag=("slot_s", "w_bf1")[half], align_bytes=64)
+            w_bf = keep.tile([P, 2, M, PACK], BF16, name="w_bf%d" % half, align_bytes=64)
             dst = w_bf[:].rearrange("p t m j -> p m t j")
             src = w_dealt[:, :, 2 * half : 2 * half + 2, :]
-            nc.vector.tensor_copy(out=dst, in_=src)
+            nc.scalar.activation(dst, src, COPY)
             w_bfs.append(w_bf)
 
         d_tab = load_words(nc.sync, "d_tab", d_words, "slot_w")
 
-        def quantise(name, values, width):
-            codes = keep.tile([P, width], U32, name=name + "_codes", align_bytes=64)
+        def quantise(name, tag, width):
+            codes = keep.tile([P, width], U32, name=name + "_codes", tag=tag, align_bytes=64)
             scales = keep.tile([P, width], U8, name=name + "_scales", align_bytes=64)
             return codes, scales
 
         def quantise_w(half):
-            codes, scales = quantise("w%d" % half, None, 2 * M)
+            codes, scales = quantise("w%d" % half, ("slot_s", "slot_x")[half], 2 * M)
             nc.vector.quantize_mx(out=codes[:].bitcast(FP8X4), scales=scales[:], in_=w_bfs[half][:].rearrange("p t m j -> p (t m j)"))
             w_codes.append(codes)
             w_scales.append(scales)
@@ -129,33 +121,39 @@ def tile_picked_hdaqsendmxpagmx_none_p_kernel(tc, x_words, x_scales, w1, gs, d_w
         d_bytes = keep.tile([P, 2 * H], U8, name="d_bytes", tag="slot_c", align_bytes=64)
         nc.vector.tensor_copy(d_bytes[:, 0:H], d_scale_tab[:].indirect(ka_t[:]))
         nc.vector.tensor_copy(d_bytes[:, H : 2 * H], d_scale_tab[:].indirect(kb_t[:]))
-        place_scale_rows(d_plane, d_bytes)
+        d_plane = place_scale_rows("d_plane", d_bytes)
         d_codes = keep.tile([P, 2 * H], U32, name="d_codes", tag="d_scale_tab", align_bytes=64)
         for side, picks in enumerate((ka_t, kb_t)):
             nc.vector.tensor_copy(d_codes[:, side * H : (side + 1) * H], d_tab[:].bitcast(U32).indirect(picks[:]))
 
         z_flat = keep.tile([P, PACK, S], BF16, name="z_flat", tag="slot_w", align_bytes=64)
         z_bf = keep.tile([P, S, PACK], BF16, name="z_bf", align_bytes=64)
-        for t in range(PACK):
+        halves = (slice(0, S // 2), slice(S // 2, S))
+        for t in range(PACK - 1):
             nc.vector.tensor_tensor(z_flat[:, t, :], ys[t][:], sent[t][:, 0:S], ALU.subtract)
-        nc.vector.tensor_copy(out=z_bf[:].rearrange("p (c i) t -> p c t i", i=4), in_=z_flat[:].rearrange("p t (c i) -> p c t i", i=4))
-        z_codes, z_scales = quantise("z", None, S)
-        nc.vector.quantize_mx(out=z_codes[:].bitcast(FP8X4), scales=z_scales[:], in_=z_bf[:].rearrange("p j t -> p (j t)"))
+        for cols in halves:
+            nc.vector.tensor_tensor(z_flat[:, PACK - 1, cols], ys[PACK - 1][:, cols], sent[PACK - 1][:, cols], ALU.subtract)
+        for cols in halves:
+            nc.vector.tensor_copy(out=z_bf[:, cols, :].rearrange("p (c i) t -> p c t i", i=4), in_=z_flat[:, :, cols].rearrange("p t (c i) -> p c t i", i=4))
+        z_codes, z_scales = quantise("z", "z_codes", S)
+        for cols in halves:
+            nc.vector.quantize_mx(out=z_codes[:, cols].bitcast(FP8X4), scales=z_scales[:, cols], in_=z_bf[:, cols, :].rearrange("p j t -> p (j t)"))
 
         for pair in range(TILES // 2):
             tiles = (2 * pair, 2 * pair + 1)
             hs, fetched, ups, dns = {}, {}, {}, {}
             for a in tiles:
-                acc = psum.tile([P, S], F32, name="h_acc%d" % a)
-                for side in range(2):
-                    nc.tensor.matmul_mx(out=acc[:], lhsT=d_codes[:, side * H + a * M : side * H + (a + 1) * M].bitcast(FP8X4),
-                                        lhsT_scale=d_plane[:, side * H + a * M : side * H + (a + 1) * M],
-                                        rhs=z_codes[:].bitcast(FP8X4), rhs_scale=z_scales[:], start=(side == 0), stop=(side == 1))
                 h = keep.tile([P, S + SPARE], F32, name="h%d" % a)
-                if a == 0:
-                    nc.scalar.activation(h[:, 0:S], acc[:], COPY, scale=0.0625)
-                else:
-                    nc.vector.tensor_scalar(h[:, 0:S], acc[:], 0.0625, None, ALU.mult)
+                for part, cols in enumerate(halves if a == 0 else (slice(0, S),)):
+                    acc = psum.tile([P, cols.stop - cols.start], F32, name="h_acc%d_%d" % (a, part), tag="y_acc0" if part == 1 else "h_acc%d" % a)
+                    for side in range(2):
+                        picked = slice(side * H + a * M, side * H + (a + 1) * M)
+                        nc.tensor.matmul_mx(out=acc[:], lhsT=d_codes[:, picked].bitcast(FP8X4), lhsT_scale=d_plane[:, picked],
+                                            rhs=z_codes[:, cols].bitcast(FP8X4), rhs_scale=z_scales[:, cols], start=(side == 0), stop=(side == 1))
+                    if a == 0:
+                        nc.scalar.activation(h[:, cols], acc[:], COPY, scale=0.0625)
+                    else:
+                        nc.vector.tensor_scalar(h[:, cols], acc[:], 0.0625, None, ALU.mult)
                 hs[a] = h
             for a in tiles:
                 fetched[a] = keep.tile([P, S], F32, name="fetched%d" % a)

@@ -47,12 +47,9 @@ def tile_picked_hdaqsendmxpagmx_none_p_kernel(tc, x_words, x_scales, w1, gs, d_w
             queue.dma_start(out=t[:], in_=src[0].rearrange("p n t -> p (n t)").bitcast(I32))
             return t
 
-        def place_scale_rows(name, picked):
-            plane = keep.tile(list(picked.shape), U8, name=name, align_bytes=64)
-            nc.vector.tensor_copy(plane[:].bitcast(I32), picked[:].bitcast(I32))
-            for b in range(2):
-                nc.sync.dma_start(out=plane[:].bitcast(I32)[2 + b : P : 32, :], in_=picked[:].bitcast(I32)[16 + b : P : 32, :])
-            return plane
+        def move_scale_rows(plane, picked, rows):
+            for i in rows:
+                nc.sync.dma_start(out=plane[:].bitcast(I32)[i:P:32, :], in_=picked[:].bitcast(I32)[16 * (i // 2) + i % 2 : P : 32, :])
 
         offs_t = load_list("offs_t", offs)
         ka_t = load_list("ka_t", ka)
@@ -68,20 +65,27 @@ def tile_picked_hdaqsendmxpagmx_none_p_kernel(tc, x_words, x_scales, w1, gs, d_w
         nc.scalar.dma_start(out=gs_t[:], in_=gs.rearrange("(p t) o -> p (t o)", t=PACK))
         x_tab = load_words(nc.scalar, "x_tab", x_words, "slot_x")
         d_scale_tab = load_scale_rows("d_scale_tab", d_scales, "d_scale_tab")
+        d_plane = keep.tile([P, 2 * H], U8, name="d_plane", align_bytes=64)
+        nc.vector.memset(d_plane[:].bitcast(I32), 0)
         pages = [keep.tile([P, U], F32, name="page%d" % a) for a in range(TILES)]
 
         x_bytes = keep.tile([P, S], U8, name="x_bytes", align_bytes=64)
         nc.vector.tensor_copy(x_bytes[:], x_scale_tab[:].indirect(offs_t[:]))
-        x_plane = place_scale_rows("x_plane", x_bytes)
+        x_plane = keep.tile([P, S], U8, name="x_plane", align_bytes=64)
+        nc.vector.tensor_copy(x_plane[:].bitcast(I32), x_bytes[:].bitcast(I32))
+        move_scale_rows(x_plane, x_bytes, (2, 3))
 
         w_dealt = w_raw[:].rearrange("p j (m t) -> p m t j", t=PACK)
         w_codes, w_scales = [], []
         w_bfs = []
         for half in range(2):
-            w_bf = keep.tile([P, 2, M, PACK], BF16, name="w_bf%d" % half, align_bytes=64)
+            w_bf = keep.tile([P, 2, M, PACK], BF16, name="w_bf%d" % half, tag=("slot_s", "w_bf1")[half], align_bytes=64)
             dst = w_bf[:].rearrange("p t m j -> p m t j")
             src = w_dealt[:, :, 2 * half : 2 * half + 2, :]
-            nc.scalar.activation(dst, src, COPY)
+            if half == 0:
+                nc.vector.tensor_copy(out=dst, in_=src)
+            else:
+                nc.scalar.activation(dst, src, COPY)
             w_bfs.append(w_bf)
 
         d_tab = load_words(nc.sync, "d_tab", d_words, "slot_w")
@@ -91,22 +95,25 @@ def tile_picked_hdaqsendmxpagmx_none_p_kernel(tc, x_words, x_scales, w1, gs, d_w
             scales = keep.tile([P, width], U8, name=name + "_scales", align_bytes=64)
             return codes, scales
 
-        def quantise_w(half):
-            codes, scales = quantise("w%d" % half, ("slot_s", "slot_x")[half], 2 * M)
-            nc.vector.quantize_mx(out=codes[:].bitcast(FP8X4), scales=scales[:], in_=w_bfs[half][:].rearrange("p t m j -> p (t m j)"))
-            w_codes.append(codes)
-            w_scales.append(scales)
+        def quantise_w(first, count, tag):
+            codes, scales = quantise("w%d" % first, tag, count * M)
+            planes = w_bfs[first // 2][:, first % 2 : first % 2 + count]
+            nc.vector.quantize_mx(out=codes[:].bitcast(FP8X4), scales=scales[:], in_=planes.rearrange("p t m j -> p (t m j)"))
+            for t in range(count):
+                w_codes.append(codes[:, t * M : (t + 1) * M])
+                w_scales.append(scales[:, t * M : (t + 1) * M])
 
-        quantise_w(0)
-        x_codes = keep.tile([P, S], U32, name="x_codes", tag="slot_c", align_bytes=64)
+        quantise_w(0, 1, "slot_q0")
+        quantise_w(1, 1, "slot_q1")
+        x_codes = keep.tile([P, S], U32, name="x_codes", align_bytes=64)
         nc.vector.tensor_copy(x_codes[:], x_tab[:].bitcast(U32).indirect(offs_t[:]))
-        quantise_w(1)
 
         ys, sent = [], []
         for t in range(PACK):
             acc = psum.tile([P, S], F32, name="y_acc%d" % t)
-            cols = slice((t % 2) * M, (t % 2 + 1) * M)
-            nc.tensor.matmul_mx(out=acc[:], lhsT=w_codes[t // 2][:, cols].bitcast(FP8X4), lhsT_scale=w_scales[t // 2][:, cols],
+            if t == 2:
+                quantise_w(2, 2, "slot_q1")
+            nc.tensor.matmul_mx(out=acc[:], lhsT=w_codes[t].bitcast(FP8X4), lhsT_scale=w_scales[t],
                                 rhs=x_codes[:].bitcast(FP8X4), rhs_scale=x_plane[:], start=True, stop=True)
             y = keep.tile([P, S], F32, name="y%d" % t)
             if t == 0:
@@ -118,10 +125,10 @@ def tile_picked_hdaqsendmxpagmx_none_p_kernel(tc, x_words, x_scales, w1, gs, d_w
             ys.append(y)
             sent.append(ds)
 
-        d_bytes = keep.tile([P, 2 * H], U8, name="d_bytes", tag="slot_c", align_bytes=64)
+        d_bytes = keep.tile([P, 2 * H], U8, name="d_bytes", tag="slot_q0", align_bytes=64)
         nc.vector.tensor_copy(d_bytes[:, 0:H], d_scale_tab[:].indirect(ka_t[:]))
         nc.vector.tensor_copy(d_bytes[:, H : 2 * H], d_scale_tab[:].indirect(kb_t[:]))
-        d_plane = place_scale_rows("d_plane", d_bytes)
+        move_scale_rows(d_plane, d_bytes, range(4))
         d_codes = keep.tile([P, 2 * H], U32, name="d_codes", tag="d_scale_tab", align_bytes=64)
         for side, picks in enumerate((ka_t, kb_t)):
             nc.vector.tensor_copy(d_codes[:, side * H : (side + 1) * H], d_tab[:].bitcast(U32).indirect(picks[:]))

@@ -34,37 +34,33 @@ def tile_picked_hdaqsendmxpagmx_none_p_kernel(tc, x_words, x_scales, w1, gs, d_w
             nc.sync.dma_start(t[:], src)
             return t
 
-        def load_scale_rows(name, src, tag):
-            t = keep.tile([P, src.shape[2]], U8, name=name, tag=tag, align_bytes=64)
-            nc.vector.memset(t[:].bitcast(I32), 0)
-            rows = src[0].bitcast(I32).rearrange("(r b) c -> b r c", b=2)
-            for b in range(2):
-                nc.gpsimd.dma_start(out=t[:].bitcast(I32)[b:P:16, :], in_=rows[b])
-            return t
 
         def load_words(queue, name, src, tag):
             t = keep.tile([P, src.shape[2]], I32, name=name, tag=tag, align_bytes=64)
             queue.dma_start(out=t[:], in_=src[0].rearrange("p n t -> p (n t)").bitcast(I32))
             return t
 
-        def move_scale_rows(plane, picked, rows):
+        def move_scale_rows(queue, plane, picked, rows):
             for i in rows:
-                nc.sync.dma_start(out=plane[:].bitcast(I32)[i:P:32, :], in_=picked[:].bitcast(I32)[16 * (i // 2) + i % 2 : P : 32, :])
+                queue.dma_start(out=plane[:].bitcast(I32)[i:P:32, :], in_=picked[:].bitcast(I32)[8 * i : P : 32, :])
 
+        gs_t = keep.tile([P, PACK], F32, name="gs_t")
+        nc.scalar.dma_start(out=gs_t[:], in_=gs.rearrange("(p t) o -> p (t o)", t=PACK))
         offs_t = load_list("offs_t", offs)
-        ka_t = load_list("ka_t", ka)
-        kb_t = load_list("kb_t", kb)
+        x_scale_tab = keep.tile([P, T], U8, name="x_scale_tab", tag="slot_s", align_bytes=64)
+        nc.sync.dma_start(out=x_scale_tab[:].bitcast(I32), in_=x_scales[0].bitcast(I32).unsqueeze(1).to_broadcast([16, 8, T // 4]))
+        w_raw = keep.tile([P, PACK, H], F32, name="w_raw", tag="slot_w", align_bytes=64)
+        nc.sync.dma_start(out=w_raw[:], in_=w1.rearrange("(p j) c -> p j c", j=PACK))
         n1_t = load_list("n1_t", n1)
+        ka_t = load_list("ka_t", ka)
+        x_tab = load_words(nc.sync, "x_tab", x_words, "x_tab")
+        kb_t = load_list("kb_t", kb)
         n4_t = load_list("n4_t", n4)
         n2_t = load_list("n2_t", n2)
         n3_t = load_list("n3_t", n3)
-        x_scale_tab = load_scale_rows("x_scale_tab", x_scales, "slot_s")
-        w_raw = keep.tile([P, PACK, H], F32, name="w_raw", tag="slot_w", align_bytes=64)
-        nc.scalar.dma_start(out=w_raw[:], in_=w1.rearrange("(p j) c -> p j c", j=PACK))
-        gs_t = keep.tile([P, PACK], F32, name="gs_t")
-        nc.scalar.dma_start(out=gs_t[:], in_=gs.rearrange("(p t) o -> p (t o)", t=PACK))
-        x_tab = load_words(nc.scalar, "x_tab", x_words, "slot_x")
-        d_scale_tab = load_scale_rows("d_scale_tab", d_scales, "d_scale_tab")
+        d_scale_tab = keep.tile([P, G], U8, name="d_scale_tab", align_bytes=64)
+        nc.vector.memset(d_scale_tab[:].bitcast(I32), 0)
+        nc.gpsimd.dma_start(out=d_scale_tab[:].bitcast(I32)[0:P:8, :], in_=d_scales[0].bitcast(I32))
         d_plane = keep.tile([P, 2 * H], U8, name="d_plane", align_bytes=64)
         nc.vector.memset(d_plane[:].bitcast(I32), 0)
         pages = [keep.tile([P, U], F32, name="page%d" % a) for a in range(TILES)]
@@ -73,46 +69,39 @@ def tile_picked_hdaqsendmxpagmx_none_p_kernel(tc, x_words, x_scales, w1, gs, d_w
         nc.vector.tensor_copy(x_bytes[:], x_scale_tab[:].indirect(offs_t[:]))
         x_plane = keep.tile([P, S], U8, name="x_plane", align_bytes=64)
         nc.vector.tensor_copy(x_plane[:].bitcast(I32), x_bytes[:].bitcast(I32))
-        move_scale_rows(x_plane, x_bytes, (2, 3))
+        move_scale_rows(nc.scalar, x_plane, x_bytes, (1, 2, 3))
 
         w_dealt = w_raw[:].rearrange("p j (m t) -> p m t j", t=PACK)
         w_codes, w_scales = [], []
-        w_bfs = []
-        for half in range(2):
-            w_bf = keep.tile([P, 2, M, PACK], BF16, name="w_bf%d" % half, tag=("slot_s", "w_bf1")[half], align_bytes=64)
-            dst = w_bf[:].rearrange("p t m j -> p m t j")
-            src = w_dealt[:, :, 2 * half : 2 * half + 2, :]
-            if half == 0:
-                nc.vector.tensor_copy(out=dst, in_=src)
-            else:
-                nc.scalar.activation(dst, src, COPY)
-            w_bfs.append(w_bf)
-
-        d_tab = load_words(nc.sync, "d_tab", d_words, "slot_w")
 
         def quantise(name, tag, width):
             codes = keep.tile([P, width], U32, name=name + "_codes", tag=tag, align_bytes=64)
             scales = keep.tile([P, width], U8, name=name + "_scales", align_bytes=64)
             return codes, scales
 
-        def quantise_w(first, count, tag):
-            codes, scales = quantise("w%d" % first, tag, count * M)
-            planes = w_bfs[first // 2][:, first % 2 : first % 2 + count]
+        def round_w(half, tag):
+            w_bf = keep.tile([P, 2, M, PACK], BF16, name="w_bf%d" % half, tag=tag, align_bytes=64)
+            nc.vector.tensor_copy(out=w_bf[:].rearrange("p t m j -> p m t j"), in_=w_dealt[:, :, 2 * half : 2 * half + 2, :])
+            return w_bf
+
+        def quantise_w(name, planes, count, tag):
+            codes, scales = quantise(name, tag, count * M)
             nc.vector.quantize_mx(out=codes[:].bitcast(FP8X4), scales=scales[:], in_=planes.rearrange("p t m j -> p (t m j)"))
             for t in range(count):
                 w_codes.append(codes[:, t * M : (t + 1) * M])
                 w_scales.append(scales[:, t * M : (t + 1) * M])
 
-        quantise_w(0, 1, "slot_q0")
-        quantise_w(1, 1, "slot_q1")
-        x_codes = keep.tile([P, S], U32, name="x_codes", align_bytes=64)
+        w_low = round_w(0, "slot_s")
+        w_high = round_w(1, "w_high")
+        quantise_w("w01", w_low[:], 2, "w01_codes")
+        quantise_w("w23", w_high[:], 2, "w23_codes")
+        d_tab = load_words(nc.sync, "d_tab", d_words, "slot_w")
+        x_codes = keep.tile([P, S], U32, name="x_codes", tag="slot_c", align_bytes=64)
         nc.vector.tensor_copy(x_codes[:], x_tab[:].bitcast(U32).indirect(offs_t[:]))
 
         ys, sent = [], []
         for t in range(PACK):
             acc = psum.tile([P, S], F32, name="y_acc%d" % t)
-            if t == 2:
-                quantise_w(2, 2, "slot_q1")
             nc.tensor.matmul_mx(out=acc[:], lhsT=w_codes[t].bitcast(FP8X4), lhsT_scale=w_scales[t],
                                 rhs=x_codes[:].bitcast(FP8X4), rhs_scale=x_plane[:], start=True, stop=True)
             y = keep.tile([P, S], F32, name="y%d" % t)
@@ -125,26 +114,28 @@ def tile_picked_hdaqsendmxpagmx_none_p_kernel(tc, x_words, x_scales, w1, gs, d_w
             ys.append(y)
             sent.append(ds)
 
-        d_bytes = keep.tile([P, 2 * H], U8, name="d_bytes", tag="slot_q0", align_bytes=64)
+        d_bytes = keep.tile([P, 2 * H], U8, name="d_bytes", tag="slot_c", align_bytes=64)
         nc.vector.tensor_copy(d_bytes[:, 0:H], d_scale_tab[:].indirect(ka_t[:]))
         nc.vector.tensor_copy(d_bytes[:, H : 2 * H], d_scale_tab[:].indirect(kb_t[:]))
-        move_scale_rows(d_plane, d_bytes, range(4))
+        move_scale_rows(nc.sync, d_plane, d_bytes, range(4))
         d_codes = keep.tile([P, 2 * H], U32, name="d_codes", tag="d_scale_tab", align_bytes=64)
         for side, picks in enumerate((ka_t, kb_t)):
             nc.vector.tensor_copy(d_codes[:, side * H : (side + 1) * H], d_tab[:].bitcast(U32).indirect(picks[:]))
 
-        z_flat = keep.tile([P, PACK, S], BF16, name="z_flat", tag="slot_w", align_bytes=64)
-        z_bf = keep.tile([P, S, PACK], BF16, name="z_bf", align_bytes=64)
+        z_pairs = keep.tile([P, 2, S, 2], BF16, name="z_pairs", tag="slot_w", align_bytes=64)
         halves = (slice(0, S // 2), slice(S // 2, S))
-        for t in range(PACK - 1):
-            nc.vector.tensor_tensor(z_flat[:, t, :], ys[t][:], sent[t][:, 0:S], ALU.subtract)
-        for cols in halves:
-            nc.vector.tensor_tensor(z_flat[:, PACK - 1, cols], ys[PACK - 1][:, cols], sent[PACK - 1][:, cols], ALU.subtract)
-        for cols in halves:
-            nc.vector.tensor_copy(out=z_bf[:, cols, :].rearrange("p (c i) t -> p c t i", i=4), in_=z_flat[:, :, cols].rearrange("p t (c i) -> p c t i", i=4))
+        for t in range(PACK):
+            for cols in halves if t == PACK - 1 else (slice(0, S),):
+                nc.vector.tensor_tensor(z_pairs[:, t // 2, cols, t % 2], ys[t][:, cols], sent[t][:, cols], ALU.subtract)
+        z_words = z_pairs[:].rearrange("p u j e -> p u (j e)").bitcast(F32)
+        z_bfs = []
+        for part, cols in enumerate(halves):
+            z_bf = keep.tile([P, 2 * S], BF16, name="z_bf%d" % part, align_bytes=64)
+            nc.vector.tensor_copy(out=z_bf[:].bitcast(F32).rearrange("p (j u) -> p j u", u=2), in_=z_words[:, :, cols].rearrange("p u j -> p j u"))
+            z_bfs.append(z_bf)
         z_codes, z_scales = quantise("z", "z_codes", S)
-        for cols in halves:
-            nc.vector.quantize_mx(out=z_codes[:, cols].bitcast(FP8X4), scales=z_scales[:, cols], in_=z_bf[:, cols, :].rearrange("p j t -> p (j t)"))
+        for part, cols in enumerate(halves):
+            nc.vector.quantize_mx(out=z_codes[:, cols].bitcast(FP8X4), scales=z_scales[:, cols], in_=z_bfs[part][:])
 
         for pair in range(TILES // 2):
             tiles = (2 * pair, 2 * pair + 1)

from contextlib import ExitStack

import concourse.mybir as mybir

K, T, S, H, G, U = 512, 2048, 256, 512, 2048, 512
FLOPS = 2 * K * H * S * 3

F32 = mybir.dt.float32
BF16 = mybir.dt.bfloat16
I32 = mybir.dt.int32
U32 = mybir.dt.uint32
U16 = mybir.dt.uint16
U8 = mybir.dt.uint8
FP8X4 = mybir.dt.float8_e4m3fn_x4
ALU = mybir.AluOpType
COPY = mybir.ActivationFunctionType.Copy

P = 128
PACK = 4
M = 128
TILES = H // M
SPARE = 16


def tile_picked_hdaqsendmxpagmx_none_p_kernel(tc, x_words, x_scales, w1, gs, d_words, d_scales, offs, n1, ka, kb, n2, n3, n4, out):
    nc = tc.nc
    with ExitStack() as ctx:
        lists = ctx.enter_context(tc.tile_pool(name="lists", bufs=1))
        keep = ctx.enter_context(tc.tile_pool(name="keep", bufs=1))
        psum = ctx.enter_context(tc.psum_pool(name="psum", bufs=1))

        def load_list(name, src):
            t = lists.tile(list(src.shape), U16, name=name)
            nc.sync.dma_start(t[:], src)
            return t


        def load_words(queue, name, src, tag):
            t = keep.tile([P, src.shape[2]], I32, name=name, tag=tag, align_bytes=64)
            queue.dma_start(out=t[:], in_=src[0].rearrange("p n t -> p (n t)").bitcast(I32))
            return t

        def move_scale_rows(queue, plane, picked, rows):
            for i in rows:
                queue.dma_start(out=plane[:].bitcast(I32)[i:P:32, :], in_=picked[:].bitcast(I32)[8 * i : P : 32, :])

        gs_t = keep.tile([P, PACK], F32, name="gs_t")
        nc.scalar.dma_start(out=gs_t[:], in_=gs.rearrange("(p t) o -> p (t o)", t=PACK))
        offs_t = load_list("offs_t", offs)
        x_scale_tab = keep.tile([P, T], U8, name="x_scale_tab", tag="slot_s", align_bytes=64)
        nc.sync.dma_start(out=x_scale_tab[:].bitcast(I32), in_=x_scales[0].bitcast(I32).unsqueeze(1).to_broadcast([16, 8, T // 4]))
        w_raw = keep.tile([P, PACK, H], F32, name="w_raw", tag="slot_w", align_bytes=64)
        nc.sync.dma_start(out=w_raw[:], in_=w1.rearrange("(p j) c -> p j c", j=PACK))
        n1_t = load_list("n1_t", n1)
        ka_t = load_list("ka_t", ka)
        x_tab = load_words(nc.sync, "x_tab", x_words, "x_tab")
        kb_t = load_list("kb_t", kb)
        n4_t = load_list("n4_t", n4)
        n2_t = load_list("n2_t", n2)
        n3_t = load_list("n3_t", n3)
        d_scale_tab = keep.tile([P, G], U8, name="d_scale_tab", align_bytes=64)
        nc.vector.memset(d_scale_tab[:].bitcast(I32), 0)
        nc.gpsimd.dma_start(out=d_scale_tab[:].bitcast(I32)[0:P:8, :], in_=d_scales[0].bitcast(I32))
        d_plane = keep.tile([P, 2 * H], U8, name="d_plane", align_bytes=64)
        nc.vector.memset(d_plane[:].bitcast(I32), 0)
        pages = [keep.tile([P, U], F32, name="page%d" % a) for a in range(TILES)]

        x_bytes = keep.tile([P, S], U8, name="x_bytes", align_bytes=64)
        nc.vector.tensor_copy(x_bytes[:], x_scale_tab[:].indirect(offs_t[:]))
        x_plane = keep.tile([P, S], U8, name="x_plane", align_bytes=64)
        nc.vector.tensor_copy(x_plane[:].bitcast(I32), x_bytes[:].bitcast(I32))
        move_scale_rows(nc.scalar, x_plane, x_bytes, (1, 2, 3))

        w_dealt = w_raw[:].rearrange("p j (m t) -> p m t j", t=PACK)
        w_codes, w_scales = [], []

        def quantise(name, tag, width):
            codes = keep.tile([P, width], U32, name=name + "_codes", tag=tag, align_bytes=64)
            scales = keep.tile([P, width], U8, name=name + "_scales", align_bytes=64)
            return codes, scales

        def round_w(half, tag):
            w_bf = keep.tile([P, 2, M, PACK], BF16, name="w_bf%d" % half, tag=tag, align_bytes=64)
            nc.vector.tensor_copy(out=w_bf[:].rearrange("p t m j -> p m t j"), in_=w_dealt[:, :, 2 * half : 2 * half + 2, :])
            return w_bf

        def quantise_w(name, planes, count, tag):
            codes, scales = quantise(name, tag, count * M)
            nc.vector.quantize_mx(out=codes[:].bitcast(FP8X4), scales=scales[:], in_=planes.rearrange("p t m j -> p (t m j)"))
            for t in range(count):
                w_codes.append(codes[:, t * M : (t + 1) * M])
                w_scales.append(scales[:, t * M : (t + 1) * M])

        w_low = round_w(0, "slot_s")
        w_high = round_w(1, "w_high")
        quantise_w("w01", w_low[:], 2, "w01_codes")
        quantise_w("w23", w_high[:], 2, "w23_codes")
        d_tab = load_words(nc.sync, "d_tab", d_words, "slot_w")
        x_codes = keep.tile([P, S], U32, name="x_codes", tag="slot_c", align_bytes=64)
        nc.vector.tensor_copy(x_codes[:], x_tab[:].bitcast(U32).indirect(offs_t[:]))

        ys, sent = [], []
        for t in range(PACK):
            acc = psum.tile([P, S], F32, name="y_acc%d" % t)
            nc.tensor.matmul_mx(out=acc[:], lhsT=w_codes[t].bitcast(FP8X4), lhsT_scale=w_scales[t],
                                rhs=x_codes[:].bitcast(FP8X4), rhs_scale=x_plane[:], start=True, stop=True)
            y = keep.tile([P, S], F32, name="y%d" % t)
            if t == 0:
                nc.scalar.activation(y[:], acc[:], COPY, scale=gs_t[:, t : t + 1])
            else:
                nc.vector.tensor_scalar(y[:], acc[:], gs_t[:, t : t + 1], None, ALU.mult)
            ds = keep.tile([P, 2 * S], F32, name="ds%d" % t)
            nc.scalar.activation(ds[:].indirect(n1_t[:]), y[:], COPY)
            ys.append(y)
            sent.append(ds)

        d_bytes = keep.tile([P, 2 * H], U8, name="d_bytes", tag="slot_c", align_bytes=64)
        nc.vector.tensor_copy(d_bytes[:, 0:H], d_scale_tab[:].indirect(ka_t[:]))
        nc.vector.tensor_copy(d_bytes[:, H : 2 * H], d_scale_tab[:].indirect(kb_t[:]))
        move_scale_rows(nc.sync, d_plane, d_bytes, range(4))
        d_codes = keep.tile([P, 2 * H], U32, name="d_codes", tag="d_scale_tab", align_bytes=64)
        for side, picks in enumerate((ka_t, kb_t)):
            nc.vector.tensor_copy(d_codes[:, side * H : (side + 1) * H], d_tab[:].bitcast(U32).indirect(picks[:]))

        z_pairs = keep.tile([P, 2, S, 2], BF16, name="z_pairs", tag="slot_w", align_bytes=64)
        halves = (slice(0, S // 2), slice(S // 2, S))
        for t in range(PACK):
            for cols in halves if t == PACK - 1 else (slice(0, S),):
                nc.vector.tensor_tensor(z_pairs[:, t // 2, cols, t % 2], ys[t][:, cols], sent[t][:, cols], ALU.subtract)
        z_words = z_pairs[:].rearrange("p u j e -> p u (j e)").bitcast(F32)
        z_bfs = []
        for part, cols in enumerate(halves):
            z_bf = keep.tile([P, 2 * S], BF16, name="z_bf%d" % part, align_bytes=64)
            nc.vector.tensor_copy(out=z_bf[:].bitcast(F32).rearrange("p (j u) -> p j u", u=2), in_=z_words[:, :, cols].rearrange("p u j -> p j u"))
            z_bfs.append(z_bf)
        z_codes, z_scales = quantise("z", "z_codes", S)
        for part, cols in enumerate(halves):
            nc.vector.quantize_mx(out=z_codes[:, cols].bitcast(FP8X4), scales=z_scales[:, cols], in_=z_bfs[part][:])

        for pair in range(TILES // 2):
            tiles = (2 * pair, 2 * pair + 1)
            hs, fetched, ups, dns = {}, {}, {}, {}
            for a in tiles:
                h = keep.tile([P, S + SPARE], F32, name="h%d" % a)
                for part, cols in enumerate(halves if a == 0 else (slice(0, S),)):
                    acc = psum.tile([P, cols.stop - cols.start], F32, name="h_acc%d_%d" % (a, part), tag="y_acc0" if part == 1 else "h_acc%d" % a)
                    for side in range(2):
                        picked = slice(side * H + a * M, side * H + (a + 1) * M)
                        nc.tensor.matmul_mx(out=acc[:], lhsT=d_codes[:, picked].bitcast(FP8X4), lhsT_scale=d_plane[:, picked],
                                            rhs=z_codes[:, cols].bitcast(FP8X4), rhs_scale=z_scales[:, cols], start=(side == 0), stop=(side == 1))
                    if a == 0:
                        nc.scalar.activation(h[:, cols], acc[:], COPY, scale=0.0625)
                    else:
                        nc.vector.tensor_scalar(h[:, cols], acc[:], 0.0625, None, ALU.mult)
                hs[a] = h
            for a in tiles:
                fetched[a] = keep.tile([P, S], F32, name="fetched%d" % a)
                nc.scalar.activation(fetched[a][:], hs[a][:].indirect(n4_t[:]), COPY)
            for a in tiles:
                ups[a] = keep.tile([P, S], F32, name="up%d" % a)
                nc.vector.tensor_tensor(ups[a][:], hs[a][:, 0:S], fetched[a][:], ALU.max)
            for a in tiles:
                dns[a] = keep.tile([P, S], F32, name="dn%d" % a)
                nc.vector.tensor_tensor(dns[a][:], hs[a][:, 0:S], fetched[a][:], ALU.min)
            for a in tiles:
                nc.scalar.activation(pages[a][:].indirect(n2_t[:]), ups[a][:], COPY)
            for a in tiles:
                nc.scalar.activation(pages[a][:].indirect(n3_t[:]), dns[a][:], COPY)
                nc.sync.dma_start(out=out[a * M : (a + 1) * M, :], in_=pages[a][:])
